import numpy as np
import ml_dtypes


def mxq(x, axis, fmt="e4m3"):
    dtype, down = {"e4m3": (ml_dtypes.float8_e4m3fn, 7), "e5m2": (ml_dtypes.float8_e5m2, 14)}[fmt]
    v = np.moveaxis(np.asarray(x, np.float32).astype(ml_dtypes.bfloat16).astype(np.float64), axis, -1)
    blocks = v.reshape(v.shape[:-1] + (-1, 32))
    amax = np.abs(blocks).max(-1, keepdims=True)
    byte = np.maximum(np.where(amax > 0, np.frexp(amax)[1] - 1 + 127, 0) - down, 1)
    scale = np.exp2(byte - 127.0)
    codes = (blocks / scale).astype(np.float32).astype(dtype).astype(np.float64)
    return np.moveaxis((codes * scale).reshape(v.shape), -1, axis)


WIDE = False


def mx_kscale(k):
    if not WIDE:
        return np.ones(k)
    levels = np.array([10, -10, 5, -5, 0])
    if k % 512:
        return np.exp2(np.random.permutation(np.resize(levels, k // 32))).repeat(32)
    a = np.empty((k // 512, 16))
    for p in range(k // 512):
        a[p, :8] = np.random.permutation(np.resize(levels, 8))
        for g in range(8):
            far = levels[np.abs(levels - a[p, g]) >= 10]
            a[p, g + 8] = far[np.random.randint(len(far))]
    return np.exp2(a.ravel()).repeat(32)


def f64(x):
    return np.asarray(x).astype(np.float64)


def striped(idx):
    return np.tile(idx.reshape(-1, 16).T, (8, 1)).astype(np.uint16)


def unstriped(offs):
    return offs[:16].T.reshape(-1).astype(np.int64)


def striped8(idx):
    return np.concatenate([x.reshape(-1, 16).T for x in idx]).astype(np.uint16)


def runs(offs, k):
    lists = np.stack([offs[16 * r : 16 * r + 16].T.reshape(-1) for r in range(8)]).astype(np.int64)
    return lists[np.arange(k) % 512 // 64]


def pack_weight(w):
    k, n = w.shape
    w = f64(np.asarray(w, np.float32).astype(ml_dtypes.bfloat16)).reshape(k // 32, 32, n)
    amax = np.abs(w).max(1)
    byte = np.clip(np.where(amax > 0, np.frexp(amax)[1] - 1 + 127 - 7, 1), 1, 254)
    scaled = (w * np.exp2(127.0 - byte)[:, None, :]).reshape(k, n).astype(np.float32)
    words = np.ascontiguousarray(scaled.reshape(k // 512, 128, 4, n).transpose(0, 1, 3, 2)).astype(ml_dtypes.float8_e4m3fn).view(np.uint8)
    return words, np.ascontiguousarray(byte.astype(np.uint8).reshape(k // 512, 16, n))


def unpack_weight(words, scales):
    g, p, n, _ = words.shape
    vals = np.ascontiguousarray(words).view(ml_dtypes.float8_e4m3fn).astype(np.float64) * np.repeat(np.exp2(scales.astype(np.float64) - 127.0), 8, axis=1)[..., None]
    return vals.transpose(0, 1, 3, 2).reshape(g * 512, n)


E2M1 = np.array([0.0, 0.5, 1.0, 1.5, 2.0, 3.0, 4.0, 6.0, -0.0, -0.5, -1.0, -1.5, -2.0, -3.0, -4.0, -6.0])


def pack_fp4(w):
    k, n = w.shape
    w = f64(np.asarray(w, np.float32).astype(ml_dtypes.bfloat16)).reshape(k // 32, 32, n)
    amax = np.abs(w).max(1)
    mant, ex = np.frexp(amax / 6.0)
    byte = np.clip(np.where(amax > 0, np.where(mant > 0.5, ex, ex - 1) + 127, 1), 1, 254)
    scaled = (w * np.exp2(127.0 - byte)[:, None, :]).reshape(k, n).astype(np.float32)
    c = np.ascontiguousarray(scaled.reshape(k // 512, 128, 4, n).transpose(0, 1, 3, 2)).astype(ml_dtypes.float4_e2m1fn).view(np.uint8) & 0xF
    words = (c[..., 0::2] | (c[..., 1::2] << 4)).reshape(k // 512, 128, 2 * n)
    return np.ascontiguousarray(words), np.ascontiguousarray(byte.astype(np.uint8).reshape(k // 512, 16, n))


def unpack_fp4(words, scales):
    g, _, n = scales.shape
    words = np.ascontiguousarray(words).reshape(g, 128, n, 2)
    nib = np.empty((g, 128, n, 4), np.uint8)
    nib[..., 0::2] = words & 0xF
    nib[..., 1::2] = words >> 4
    vals = E2M1[nib] * np.repeat(np.exp2(scales.astype(np.float64) - 127.0), 8, axis=1)[..., None]
    return vals.transpose(0, 1, 3, 2).reshape(g * 512, n)


def relu(v):
    return np.maximum(v, 0.0)

def planes(y):
    n, m = y.shape
    v = y.astype(np.float32).astype(ml_dtypes.bfloat16).astype(np.float64).reshape(n // 32, 32, m)
    top = np.abs(v).max(1)
    byte = np.clip(np.where(top > 0, np.frexp(top)[1] - 1 + 127 - 7, 1), 1, 254)
    codes = (v * np.exp2(127.0 - byte)[:, None, :]).reshape(n, m).astype(np.float32).astype(ml_dtypes.float8_e4m3fn).view(np.uint8)
    words = codes.reshape(n // 512, 128, 4, m).transpose(0, 1, 3, 2)
    return np.ascontiguousarray(words), np.ascontiguousarray(byte.astype(np.uint8).reshape(n // 512, 16, m))


K, T, S, V, H, W = 512, 2048, 512, 512, 512, 256


def setup_inputs():
    n = np.random.standard_normal
    s = mx_kscale(K)[:, None]
    u = mx_kscale(S)
    packed_xT = pack_weight(n((K, T)) * s)
    packed_w1 = pack_fp4(n((K, H)) / np.sqrt(K) / s)
    packed_w2 = pack_fp4(n((K, H)) / np.sqrt(K) / s)
    perm = np.stack([np.random.permutation(S) for _ in range(8)])
    return {
        "x_words": packed_xT[0],
        "x_scales": packed_xT[1],
        "w1_words": packed_w1[0],
        "w1_scales": packed_w1[1],
        "w2_words": packed_w2[0],
        "w2_scales": packed_w2[1],
        "ga": (np.random.uniform(0.5, 1.5, (H, 1)) * u[:, None]).astype(np.float32),
        "gb": (np.random.uniform(0.5, 1.5, (H, 1)) / u[:, None]).astype(np.float32),
        "offs": striped(np.random.permutation(T)[:S]),
        "two": striped(np.random.permutation(T)[:V]),
        "la": striped8(perm[:, :W]),
        "lb": striped8(perm[:, W:]),
        "nq": striped8(np.stack([np.random.permutation(V) for _ in range(8)])),
    }


def reference(x_words, x_scales, w1_words, w1_scales, w2_words, w2_scales, ga, gb, offs, two, la, lb, nq):
    xq = unpack_weight(x_words, x_scales)[:, unstriped(offs)]
    a = unpack_fp4(w1_words, w1_scales).T @ xq
    p = a[np.arange(H)[:, None], runs(la, H)]
    qv = a[np.arange(H)[:, None], runs(lb, H)]
    lo = np.minimum(p, qv)
    hi = np.maximum(p, qv)
    d1 = np.zeros((H, S))
    d1[np.arange(H)[:, None], runs(la, H)] = hi
    d2 = d1.copy()
    d2[np.arange(H)[:, None], runs(lb, H)] = lo
    z = f64(ga) * d2
    x_two = unpack_weight(x_words, x_scales)[:, unstriped(two)]
    b = unpack_fp4(w2_words, w2_scales).T @ x_two
    z2 = f64(gb) * (b[np.arange(H)[:, None], runs(nq, H)])
    s = 0.0625 * ((mxq(z, 0, "e4m3").T @ mxq(z2, 0, "e4m3")))
    out_0 = relu(s)
    return (out_0,) + planes(out_0)

@@ -1,0 +1,224 @@
+from contextlib import ExitStack
+
+import concourse.mybir as mybir
+from concourse.masks import make_identity
+
+F32 = mybir.dt.float32
+BF16 = mybir.dt.bfloat16
+I32 = mybir.dt.int32
+U32 = mybir.dt.uint32
+U16 = mybir.dt.uint16
+U8 = mybir.dt.uint8
+FP8X4 = mybir.dt.float8_e4m3fn_x4
+FP4X4 = mybir.dt.float4_e2m1fn_x4
+ACT = mybir.ActivationFunctionType
+ALU = mybir.AluOpType
+
+P = 128
+PACK = 4
+T = 2048
+S = 512
+W = 256
+CHUNK = 128
+FLOPS = 3 * 2 * 512 * 512 * 512
+
+
+def tile_picked_keyord_none_po_kernel(
+    tc, x_words, x_scales, w1_words, w1_scales, w2_words, w2_scales, ga, gb, offs, two, la, lb, nq, out_0, out_1, out_2
+):
+    nc = tc.nc
+    with ExitStack() as ctx:
+        keep = ctx.enter_context(tc.tile_pool(name="keep", bufs=1))
+        psum = ctx.enter_context(tc.psum_pool(name="psum", bufs=8))
+
+        def tile(name, shape, dtype, tag=None):
+            return keep.tile(shape, dtype, name=name, tag=tag or name, align_bytes=64)
+
+        def load_list(name, src):
+            dst = keep.tile([P, src.shape[1]], U16, name=name)
+            nc.sync.dma_start(dst[:], src)
+            return dst
+
+        def load_scale_rows(queue, dst_i32, src):
+            for q in range(4):
+                queue.dma_start(dst_i32[32 * q : 32 * q + 4, :], src[0, 4 * q : 4 * q + 4, :].bitcast(I32))
+
+        xs = tile("xs", [P, T], U8)
+        ws_raw = tile("ws_raw", [P, S], U8)
+        w_raw = tile("w_raw", [P, 2 * S // 4], I32)
+        nc.gpsimd.dma_start(w_raw[:], w1_words[0].bitcast(I32))
+        nc.vector.memset(xs[:].bitcast(I32), 0)
+        nc.vector.memset(ws_raw[:].bitcast(I32), 0)
+        ident = tile("ident", [P, P], F32)
+        g_rows = tile("g_rows", [P, P], F32)
+
+        offs_t = load_list("offs_t", offs)
+        load_scale_rows(nc.scalar, xs[:].bitcast(I32), x_scales)
+        two_t = load_list("two_t", two)
+        la_t = load_list("la_t", la)
+        lb_t = load_list("lb_t", lb)
+        nq_t = load_list("nq_t", nq)
+        xw = tile("xw", [P, T], I32)
+        nc.sync.dma_start(xw[:], x_words[0].rearrange("p n t -> p (n t)").bitcast(I32))
+        for q in range(4):
+            queue = nc.gpsimd if q == 3 else nc.scalar
+            queue.dma_start(ws_raw[:].bitcast(I32)[32 * q : 32 * q + 4, :], w1_scales[0, 4 * q : 4 * q + 4, :].bitcast(I32))
+        nc.gpsimd.memset(g_rows[:], 0.0)
+        make_identity(nc, ident[:])
+        for i, g in enumerate((gb, ga)):
+            nc.sync.dma_start(
+                g_rows[4 * i : 4 * i + 4, :].rearrange("t (b e) -> t b e", e=8),
+                g.rearrange("(b t e) o -> t b (e o)", t=PACK, e=8),
+            )
+
+        picked_scales = []
+        for name, lst in (("xs_a", offs_t), ("xs_b", two_t)):
+            dst = tile(name, [P, S], U8)
+            nc.vector.tensor_copy(dst[:], xs[:].indirect(lst[:]))
+            picked_scales.append(dst)
+
+        def pick_words(i, lst):
+            words = tile("xw_%d" % i, [P, S], U32)
+            nc.vector.tensor_copy(words[:], xw[:].bitcast(U32).indirect(lst[:]))
+            return words
+
+        def deal(i):
+            w_dealt = tile("w_dealt%d" % i, [P, 2 * S], U8)
+            ws_dealt = tile("ws_dealt%d" % i, [P, S], U8)
+            nc.vector.tensor_copy(
+                w_dealt[:].bitcast(I32).rearrange("p (t b e) -> p t b e", t=PACK, e=4),
+                w_raw[:].rearrange("p (b t e) -> p t b e", t=PACK, e=4),
+            )
+            nc.vector.tensor_copy(
+                ws_dealt[:].bitcast(I32).rearrange("p (t b e) -> p t b e", t=PACK, e=2),
+                ws_raw[:].bitcast(I32).rearrange("p (b t e) -> p t b e", t=PACK, e=2),
+            )
+            return w_dealt, ws_dealt
+
+        def project(i, words, w_dealt, ws_dealt):
+            banks = []
+            for t in range(PACK):
+                bank = psum.tile([P, S], F32, name="proj%d_%d" % (i, t), tag="bank")
+                nc.tensor.matmul_mx(
+                    out=bank[:],
+                    lhsT=w_dealt[:, 2 * P * t : 2 * P * (t + 1)].bitcast(FP4X4),
+                    lhsT_scale=ws_dealt[:, P * t : P * (t + 1)],
+                    rhs=words[:].bitcast(FP8X4),
+                    rhs_scale=picked_scales[i][:],
+                    start=True,
+                    stop=True,
+                )
+                banks.append(bank)
+            return banks
+
+        words_a = pick_words(0, offs_t)
+        dealt1 = deal(0)
+        a_rows = []
+        for t, bank in enumerate(project(0, words_a, *dealt1)):
+            row = tile("a_rows%d" % t, [P, S], F32)
+            nc.scalar.copy(row[:], bank[:])
+            a_rows.append(row)
+        words_b = pick_words(1, two_t)
+
+        nc.sync.dma_start(w_raw[:], w2_words[0].bitcast(I32))
+        load_scale_rows(nc.sync, ws_raw[:].bitcast(I32), w2_scales)
+        g_bank = psum.tile([P, S], F32, name="g_bank", tag="bank")
+        nc.tensor.transpose(g_bank[:, 0:P], g_rows[:], ident[:])
+        gains = tile("gains", [P, 8], F32)
+        nc.scalar.copy(gains[:], g_bank[:, 0:8])
+        b_rows = []
+
+        def project_b():
+            for t, bank in enumerate(project(1, words_b, *deal(1))):
+                row = tile("b_rows%d" % t, [P, S], F32)
+                nc.scalar.activation(row[:], bank[:], ACT.Copy, scale=gains[:, t : t + 1])
+                b_rows.append(row)
+
+        z_in = tile("z_in", [P, PACK, P, PACK], BF16)
+        for half in range(2):
+            pair = (2 * half, 2 * half + 1)
+            pq = tile("pq%d" % half, [P, 2, 2, W], F32)
+            for u, t in enumerate(pair):
+                nc.vector.tensor_copy(pq[:, 0, u, :], a_rows[t][:].indirect(la_t[:]))
+                nc.vector.tensor_copy(pq[:, 1, u, :], a_rows[t][:].indirect(lb_t[:]))
+            hl = tile("hl%d" % half, [P, 2, 2, W], F32, tag=("late" if half == 1 else None))
+            nc.vector.tensor_tensor(hl[:, 0, :, :], pq[:, 0, :, :], pq[:, 1, :, :], ALU.max)
+            nc.vector.tensor_tensor(hl[:, 1, :, :], pq[:, 0, :, :], pq[:, 1, :, :], ALU.min)
+            if half == 0:
+                project_b()
+            d = [tile("d%d" % t, [P, S], F32) for t in pair]
+            for side, lst in enumerate((la_t, lb_t)):
+                for u in range(2):
+                    nc.vector.tensor_copy(d[u][:].indirect(lst[:]), hl[:, side, u, :])
+            for u, t in enumerate(pair):
+                nc.scalar.activation(
+                    z_in[:, :, :, t].rearrange("p r m -> p m r"),
+                    d[u][:].rearrange("p (m r) -> p m r", r=PACK),
+                    ACT.Copy,
+                    scale=gains[:, PACK + t : PACK + t + 1],
+                )
+
+        n_chunks = S // CHUNK
+        fetched = tile("fetched", [P, n_chunks, PACK, CHUNK], BF16, tag="late")
+        z_words = tile("z_words", [P, S], U32)
+        z_scales = tile("z_scales", [P, S], U8)
+        y_words = tile("y_words", [P, S], U32)
+        y_scales = tile("y_scales", [P, S], U8)
+        out_rows = out_0.rearrange("(p r) v -> p r v", r=PACK)
+        out_words = out_1[0].rearrange("p n t -> p (n t)").bitcast(I32)
+
+        def fetch(c):
+            for t in range(PACK):
+                cols = slice(c * CHUNK // 16, (c + 1) * CHUNK // 16)
+                nc.vector.tensor_copy(fetched[:, c, t, :], b_rows[t][:].indirect(nq_t[:, cols]))
+            z2_in = tile("z2_in%d" % c, [P, CHUNK, PACK], BF16)
+            nc.scalar.copy(z2_in[:], fetched[:, c, :, :].rearrange("p t n -> p n t"))
+            return z2_in
+
+        def score(c, z2_in):
+            z2_words = tile("z2_words%d" % c, [P, CHUNK], U32)
+            z2_scales = tile("z2_scales%d" % c, [P, CHUNK], U8)
+            nc.vector.quantize_mx(
+                out=z2_words[:].bitcast(FP8X4), scales=z2_scales[:], in_=z2_in[:].rearrange("p n t -> p (n t)")
+            )
+            bank = psum.tile([P, PACK, CHUNK], F32, name="score%d" % c, tag="bank")
+            for r in range(PACK):
+                nc.tensor.matmul_mx(
+                    out=bank[:, r, :],
+                    lhsT=z_words[:, P * r : P * (r + 1)].bitcast(FP8X4),
+                    lhsT_scale=z_scales[:, P * r : P * (r + 1)],
+                    rhs=z2_words[:].bitcast(FP8X4),
+                    rhs_scale=z2_scales[:],
+                    start=True,
+                    stop=True,
+                )
+            y = tile("y%d" % c, [P, PACK, CHUNK], F32)
+            nc.scalar.activation(y[:], bank[:], ACT.Relu, scale=0.0625)
+            nc.sync.dma_start(out_rows[:, :, c * CHUNK : (c + 1) * CHUNK], y[:])
+            return y
+
+        def hand_on(c, y):
+            y_in = tile("y_in%d" % c, [P, CHUNK, PACK], BF16)
+            nc.vector.tensor_copy(y_in[:], y[:].rearrange("p r n -> p n r"))
+            cols = slice(c * CHUNK, (c + 1) * CHUNK)
+            nc.vector.quantize_mx(
+                out=y_words[:, cols].bitcast(FP8X4), scales=y_scales[:, cols], in_=y_in[:].rearrange("p n t -> p (n t)")
+            )
+            nc.sync.dma_start(out_words[:, cols], y_words[:, cols].bitcast(I32))
+
+        z2_ins, y_ins = {}, {}
+        for step in range(n_chunks + 3):
+            if step < n_chunks:
+                z2_ins[step] = fetch(step)
+            if step == 1:
+                nc.vector.quantize_mx(
+                    out=z_words[:].bitcast(FP8X4), scales=z_scales[:], in_=z_in[:].rearrange("p r m t -> p (r m t)")
+                )
+            if 1 <= step <= n_chunks:
+                y_ins[step - 1] = score(step - 1, z2_ins[step - 1])
+            if step >= 3:
+                hand_on(step - 3, y_ins[step - 3])
+        for q in range(4):
+            (nc.sync if q % 2 else nc.scalar).dma_start(
+                out_2[0, 4 * q : 4 * q + 4, :].bitcast(I32), y_scales[32 * q : 32 * q + 4, :].bitcast(I32)
+            )

@@ -45,12 +45,18 @@ def tile_picked_keyord_none_po_kernel(
 
         xs = tile("xs", [P, T], U8)
         ws_raw = tile("ws_raw", [P, S], U8)
-        w_raw = tile("w_raw", [P, 2 * S // 4], I32)
-        nc.gpsimd.dma_start(w_raw[:], w1_words[0].bitcast(I32))
+        w_raw = [tile("w_raw0", [P, 2 * S // 4], I32)]
         nc.vector.memset(xs[:].bitcast(I32), 0)
         nc.vector.memset(ws_raw[:].bitcast(I32), 0)
         ident = tile("ident", [P, P], F32)
         g_rows = tile("g_rows", [P, P], F32)
+        nc.gpsimd.memset(g_rows[:], 0.0)
+        make_identity(nc, ident[:])
+        for i, g in enumerate((gb, ga)):
+            nc.gpsimd.dma_start(
+                g_rows[4 * i : 4 * i + 4, :].rearrange("t (b e) -> t b e", e=8),
+                g.rearrange("(b t e) o -> t b (e o)", t=PACK, e=8),
+            )
 
         offs_t = load_list("offs_t", offs)
         load_scale_rows(nc.scalar, xs[:].bitcast(I32), x_scales)
@@ -58,24 +64,19 @@ def tile_picked_keyord_none_po_kernel(
         la_t = load_list("la_t", la)
         lb_t = load_list("lb_t", lb)
         nq_t = load_list("nq_t", nq)
+        nc.sync.dma_start(w_raw[0][:], w1_words[0].bitcast(I32))
         xw = tile("xw", [P, T], I32)
         nc.sync.dma_start(xw[:], x_words[0].rearrange("p n t -> p (n t)").bitcast(I32))
-        for q in range(4):
-            queue = nc.gpsimd if q == 3 else nc.scalar
-            queue.dma_start(ws_raw[:].bitcast(I32)[32 * q : 32 * q + 4, :], w1_scales[0, 4 * q : 4 * q + 4, :].bitcast(I32))
-        nc.gpsimd.memset(g_rows[:], 0.0)
-        make_identity(nc, ident[:])
-        for i, g in enumerate((gb, ga)):
-            nc.sync.dma_start(
-                g_rows[4 * i : 4 * i + 4, :].rearrange("t (b e) -> t b e", e=8),
-                g.rearrange("(b t e) o -> t b (e o)", t=PACK, e=8),
-            )
+        load_scale_rows(nc.scalar, ws_raw[:].bitcast(I32), w1_scales)
 
         picked_scales = []
-        for name, lst in (("xs_a", offs_t), ("xs_b", two_t)):
-            dst = tile(name, [P, S], U8)
+
+        def pick_scales(name, lst, tag):
+            dst = tile(name, [P, S], U8, tag=tag)
             nc.vector.tensor_copy(dst[:], xs[:].indirect(lst[:]))
             picked_scales.append(dst)
+
+        pick_scales("xs_a", offs_t, None)
 
         def pick_words(i, lst):
             words = tile("xw_%d" % i, [P, S], U32)
@@ -87,7 +88,7 @@ def tile_picked_keyord_none_po_kernel(
             ws_dealt = tile("ws_dealt%d" % i, [P, S], U8)
             nc.vector.tensor_copy(
                 w_dealt[:].bitcast(I32).rearrange("p (t b e) -> p t b e", t=PACK, e=4),
-                w_raw[:].rearrange("p (b t e) -> p t b e", t=PACK, e=4),
+                w_raw[i][:].rearrange("p (b t e) -> p t b e", t=PACK, e=4),
             )
             nc.vector.tensor_copy(
                 ws_dealt[:].bitcast(I32).rearrange("p (t b e) -> p t b e", t=PACK, e=2),
@@ -118,9 +119,11 @@ def tile_picked_keyord_none_po_kernel(
             row = tile("a_rows%d" % t, [P, S], F32)
             nc.scalar.copy(row[:], bank[:])
             a_rows.append(row)
+        pick_scales("xs_b", two_t, "w_raw0")
         words_b = pick_words(1, two_t)
 
-        nc.sync.dma_start(w_raw[:], w2_words[0].bitcast(I32))
+        w_raw.append(tile("w_raw1", [P, 2 * S // 4], I32, tag="xs"))
+        nc.sync.dma_start(w_raw[1][:], w2_words[0].bitcast(I32))
         load_scale_rows(nc.sync, ws_raw[:].bitcast(I32), w2_scales)
         g_bank = psum.tile([P, S], F32, name="g_bank", tag="bank")
         nc.tensor.transpose(g_bank[:, 0:P], g_rows[:], ident[:])
@@ -135,31 +138,29 @@ def tile_picked_keyord_none_po_kernel(
                 b_rows.append(row)
 
         z_in = tile("z_in", [P, PACK, P, PACK], BF16)
-        for half in range(2):
-            pair = (2 * half, 2 * half + 1)
-            pq = tile("pq%d" % half, [P, 2, 2, W], F32)
-            for u, t in enumerate(pair):
-                nc.vector.tensor_copy(pq[:, 0, u, :], a_rows[t][:].indirect(la_t[:]))
-                nc.vector.tensor_copy(pq[:, 1, u, :], a_rows[t][:].indirect(lb_t[:]))
-            hl = tile("hl%d" % half, [P, 2, 2, W], F32, tag=("late" if half == 1 else None))
-            nc.vector.tensor_tensor(hl[:, 0, :, :], pq[:, 0, :, :], pq[:, 1, :, :], ALU.max)
-            nc.vector.tensor_tensor(hl[:, 1, :, :], pq[:, 0, :, :], pq[:, 1, :, :], ALU.min)
-            if half == 0:
-                project_b()
-            d = [tile("d%d" % t, [P, S], F32) for t in pair]
-            for side, lst in enumerate((la_t, lb_t)):
-                for u in range(2):
-                    nc.vector.tensor_copy(d[u][:].indirect(lst[:]), hl[:, side, u, :])
-            for u, t in enumerate(pair):
-                nc.scalar.activation(
-                    z_in[:, :, :, t].rearrange("p r m -> p m r"),
-                    d[u][:].rearrange("p (m r) -> p m r", r=PACK),
-                    ACT.Copy,
-                    scale=gains[:, PACK + t : PACK + t + 1],
-                )
+        p_vals = tile("p_vals", [P, PACK, W], F32)
+        q_vals = tile("q_vals", [P, PACK, W], F32)
+        for t in range(PACK):
+            nc.vector.tensor_copy(p_vals[:, t, :], a_rows[t][:].indirect(la_t[:]))
+            nc.vector.tensor_copy(q_vals[:, t, :], a_rows[t][:].indirect(lb_t[:]))
+        project_b()
+        hi = tile("hi", [P, PACK, W], F32, tag="ring0")
+        lo = tile("lo", [P, PACK, W], F32, tag="ring1")
+        nc.vector.tensor_tensor(hi[:], p_vals[:], q_vals[:], ALU.max)
+        nc.vector.tensor_tensor(lo[:], p_vals[:], q_vals[:], ALU.min)
+        d = [tile("d%d" % t, [P, S], F32) for t in range(PACK)]
+        for t in range(PACK):
+            nc.vector.tensor_copy(d[t][:].indirect(la_t[:]), hi[:, t, :])
+        for t in range(PACK):
+            nc.vector.tensor_copy(d[t][:].indirect(lb_t[:]), lo[:, t, :])
+            nc.scalar.activation(
+                z_in[:, :, :, t].rearrange("p r m -> p m r"),
+                d[t][:].rearrange("p (m r) -> p m r", r=PACK),
+                ACT.Copy,
+                scale=gains[:, PACK + t : PACK + t + 1],
+            )
 
         n_chunks = S // CHUNK
-        fetched = tile("fetched", [P, n_chunks, PACK, CHUNK], BF16, tag="late")
         z_words = tile("z_words", [P, S], U32)
         z_scales = tile("z_scales", [P, S], U8)
         y_words = tile("y_words", [P, S], U32)
@@ -168,11 +169,12 @@ def tile_picked_keyord_none_po_kernel(
         out_words = out_1[0].rearrange("p n t -> p (n t)").bitcast(I32)
 
         def fetch(c):
+            fetched = tile("fetched%d" % c, [P, PACK, CHUNK], BF16, tag="ring%d" % (c % 2))
             for t in range(PACK):
                 cols = slice(c * CHUNK // 16, (c + 1) * CHUNK // 16)
-                nc.vector.tensor_copy(fetched[:, c, t, :], b_rows[t][:].indirect(nq_t[:, cols]))
+                nc.vector.tensor_copy(fetched[:, t, :], b_rows[t][:].indirect(nq_t[:, cols]))
             z2_in = tile("z2_in%d" % c, [P, CHUNK, PACK], BF16)
-            nc.scalar.copy(z2_in[:], fetched[:, c, :, :].rearrange("p t n -> p n t"))
+            nc.scalar.copy(z2_in[:], fetched[:].rearrange("p t n -> p n t"))
             return z2_in
 
         def score(c, z2_in):
@@ -206,18 +208,17 @@ def tile_picked_keyord_none_po_kernel(
             )
             nc.sync.dma_start(out_words[:, cols], y_words[:, cols].bitcast(I32))
 
-        z2_ins, y_ins = {}, {}
-        for step in range(n_chunks + 3):
-            if step < n_chunks:
-                z2_ins[step] = fetch(step)
-            if step == 1:
-                nc.vector.quantize_mx(
-                    out=z_words[:].bitcast(FP8X4), scales=z_scales[:], in_=z_in[:].rearrange("p r m t -> p (r m t)")
-                )
-            if 1 <= step <= n_chunks:
-                y_ins[step - 1] = score(step - 1, z2_ins[step - 1])
-            if step >= 3:
-                hand_on(step - 3, y_ins[step - 3])
+        z2_ins = [fetch(0), fetch(1)]
+        nc.vector.quantize_mx(
+            out=z_words[:].bitcast(FP8X4), scales=z_scales[:], in_=z_in[:].rearrange("p r m t -> p (r m t)")
+        )
+        ys = []
+        for c in range(n_chunks):
+            ys.append(score(c, z2_ins[c]))
+            if c + 2 < n_chunks:
+                z2_ins.append(fetch(c + 2))
+        for c in range(n_chunks):
+            hand_on(c, ys[c])
         for q in range(4):
             (nc.sync if q % 2 else nc.scalar).dma_start(
                 out_2[0, 4 * q : 4 * q + 4, :].bitcast(I32), y_scales[32 * q : 32 * q + 4, :].bitcast(I32)

from contextlib import ExitStack

import concourse.mybir as mybir
from concourse.masks import make_identity

F32 = mybir.dt.float32
BF16 = mybir.dt.bfloat16
I32 = mybir.dt.int32
U32 = mybir.dt.uint32
U16 = mybir.dt.uint16
U8 = mybir.dt.uint8
FP8X4 = mybir.dt.float8_e4m3fn_x4
FP4X4 = mybir.dt.float4_e2m1fn_x4
ACT = mybir.ActivationFunctionType
ALU = mybir.AluOpType

P = 128
PACK = 4
T = 2048
S = 512
W = 256
CHUNK = 128
FLOPS = 3 * 2 * 512 * 512 * 512


def tile_picked_keyord_none_po_kernel(
    tc, x_words, x_scales, w1_words, w1_scales, w2_words, w2_scales, ga, gb, offs, two, la, lb, nq, out_0, out_1, out_2
):
    nc = tc.nc
    with ExitStack() as ctx:
        keep = ctx.enter_context(tc.tile_pool(name="keep", bufs=1))
        psum = ctx.enter_context(tc.psum_pool(name="psum", bufs=8))

        def tile(name, shape, dtype, tag=None):
            return keep.tile(shape, dtype, name=name, tag=tag or name, align_bytes=64)

        def load_list(name, src):
            dst = keep.tile([P, src.shape[1]], U16, name=name)
            nc.sync.dma_start(dst[:], src)
            return dst

        def load_scale_rows(queue, dst_i32, src):
            for q in range(4):
                queue.dma_start(dst_i32[32 * q : 32 * q + 4, :], src[0, 4 * q : 4 * q + 4, :].bitcast(I32))

        xs = tile("xs", [P, T], U8)
        ws_raw = tile("ws_raw", [P, S], U8)
        w_raw = [tile("w_raw0", [P, 2 * S // 4], I32)]
        nc.vector.memset(xs[:].bitcast(I32), 0)
        nc.vector.memset(ws_raw[:].bitcast(I32), 0)
        ident = tile("ident", [P, P], F32)
        g_rows = tile("g_rows", [P, P], F32)
        nc.gpsimd.memset(g_rows[:], 0.0)
        make_identity(nc, ident[:])
        for i, g in enumerate((gb, ga)):
            nc.gpsimd.dma_start(
                g_rows[4 * i : 4 * i + 4, :].rearrange("t (b e) -> t b e", e=8),
                g.rearrange("(b t e) o -> t b (e o)", t=PACK, e=8),
            )

        offs_t = load_list("offs_t", offs)
        load_scale_rows(nc.scalar, xs[:].bitcast(I32), x_scales)
        two_t = load_list("two_t", two)
        la_t = load_list("la_t", la)
        lb_t = load_list("lb_t", lb)
        nq_t = load_list("nq_t", nq)
        nc.sync.dma_start(w_raw[0][:], w1_words[0].bitcast(I32))
        xw = tile("xw", [P, T], I32)
        nc.sync.dma_start(xw[:], x_words[0].rearrange("p n t -> p (n t)").bitcast(I32))
        load_scale_rows(nc.scalar, ws_raw[:].bitcast(I32), w1_scales)

        picked_scales = []

        def pick_scales(name, lst, tag):
            dst = tile(name, [P, S], U8, tag=tag)
            nc.vector.tensor_copy(dst[:], xs[:].indirect(lst[:]))
            picked_scales.append(dst)

        pick_scales("xs_a", offs_t, None)

        def pick_words(i, lst):
            words = tile("xw_%d" % i, [P, S], U32)
            nc.vector.tensor_copy(words[:], xw[:].bitcast(U32).indirect(lst[:]))
            return words

        def deal(i):
            w_dealt = tile("w_dealt%d" % i, [P, 2 * S], U8)
            ws_dealt = tile("ws_dealt%d" % i, [P, S], U8)
            nc.vector.tensor_copy(
                w_dealt[:].bitcast(I32).rearrange("p (t b e) -> p t b e", t=PACK, e=4),
                w_raw[i][:].rearrange("p (b t e) -> p t b e", t=PACK, e=4),
            )
            nc.vector.tensor_copy(
                ws_dealt[:].bitcast(I32).rearrange("p (t b e) -> p t b e", t=PACK, e=2),
                ws_raw[:].bitcast(I32).rearrange("p (b t e) -> p t b e", t=PACK, e=2),
            )
            return w_dealt, ws_dealt

        def project(i, words, w_dealt, ws_dealt):
            banks = []
            for t in range(PACK):
                bank = psum.tile([P, S], F32, name="proj%d_%d" % (i, t), tag="bank")
                nc.tensor.matmul_mx(
                    out=bank[:],
                    lhsT=w_dealt[:, 2 * P * t : 2 * P * (t + 1)].bitcast(FP4X4),
                    lhsT_scale=ws_dealt[:, P * t : P * (t + 1)],
                    rhs=words[:].bitcast(FP8X4),
                    rhs_scale=picked_scales[i][:],
                    start=True,
                    stop=True,
                )
                banks.append(bank)
            return banks

        words_a = pick_words(0, offs_t)
        dealt1 = deal(0)
        a_rows = []
        for t, bank in enumerate(project(0, words_a, *dealt1)):
            row = tile("a_rows%d" % t, [P, S], F32)
            nc.scalar.copy(row[:], bank[:])
            a_rows.append(row)
        pick_scales("xs_b", two_t, "w_raw0")
        words_b = pick_words(1, two_t)

        w_raw.append(tile("w_raw1", [P, 2 * S // 4], I32, tag="xs"))
        nc.sync.dma_start(w_raw[1][:], w2_words[0].bitcast(I32))
        load_scale_rows(nc.sync, ws_raw[:].bitcast(I32), w2_scales)
        g_bank = psum.tile([P, S], F32, name="g_bank", tag="bank")
        nc.tensor.transpose(g_bank[:, 0:P], g_rows[:], ident[:])
        gains = tile("gains", [P, 8], F32)
        nc.scalar.copy(gains[:], g_bank[:, 0:8])
        b_rows = []

        def project_b():
            for t, bank in enumerate(project(1, words_b, *deal(1))):
                row = tile("b_rows%d" % t, [P, S], F32)
                nc.scalar.activation(row[:], bank[:], ACT.Copy, scale=gains[:, t : t + 1])
                b_rows.append(row)

        z_in = tile("z_in", [P, PACK, P, PACK], BF16)
        p_vals = tile("p_vals", [P, PACK, W], F32)
        q_vals = tile("q_vals", [P, PACK, W], F32)
        for t in range(PACK):
            nc.vector.tensor_copy(p_vals[:, t, :], a_rows[t][:].indirect(la_t[:]))
            nc.vector.tensor_copy(q_vals[:, t, :], a_rows[t][:].indirect(lb_t[:]))
        project_b()
        hi = tile("hi", [P, PACK, W], F32, tag="ring0")
        lo = tile("lo", [P, PACK, W], F32, tag="ring1")
        nc.vector.tensor_tensor(hi[:], p_vals[:], q_vals[:], ALU.max)
        nc.vector.tensor_tensor(lo[:], p_vals[:], q_vals[:], ALU.min)
        d = [tile("d%d" % t, [P, S], F32) for t in range(PACK)]
        for t in range(PACK):
            nc.vector.tensor_copy(d[t][:].indirect(la_t[:]), hi[:, t, :])
        for t in range(PACK):
            nc.vector.tensor_copy(d[t][:].indirect(lb_t[:]), lo[:, t, :])
            nc.scalar.activation(
                z_in[:, :, :, t].rearrange("p r m -> p m r"),
                d[t][:].rearrange("p (m r) -> p m r", r=PACK),
                ACT.Copy,
                scale=gains[:, PACK + t : PACK + t + 1],
            )

        n_chunks = S // CHUNK
        z_words = tile("z_words", [P, S], U32)
        z_scales = tile("z_scales", [P, S], U8)
        y_words = tile("y_words", [P, S], U32)
        y_scales = tile("y_scales", [P, S], U8)
        out_rows = out_0.rearrange("(p r) v -> p r v", r=PACK)
        out_words = out_1[0].rearrange("p n t -> p (n t)").bitcast(I32)

        def fetch(c):
            fetched = tile("fetched%d" % c, [P, PACK, CHUNK], BF16, tag="ring%d" % (c % 2))
            for t in range(PACK):
                cols = slice(c * CHUNK // 16, (c + 1) * CHUNK // 16)
                nc.vector.tensor_copy(fetched[:, t, :], b_rows[t][:].indirect(nq_t[:, cols]))
            z2_in = tile("z2_in%d" % c, [P, CHUNK, PACK], BF16)
            nc.scalar.copy(z2_in[:], fetched[:].rearrange("p t n -> p n t"))
            return z2_in

        def score(c, z2_in):
            z2_words = tile("z2_words%d" % c, [P, CHUNK], U32)
            z2_scales = tile("z2_scales%d" % c, [P, CHUNK], U8)
            nc.vector.quantize_mx(
                out=z2_words[:].bitcast(FP8X4), scales=z2_scales[:], in_=z2_in[:].rearrange("p n t -> p (n t)")
            )
            bank = psum.tile([P, PACK, CHUNK], F32, name="score%d" % c, tag="bank")
            for r in range(PACK):
                nc.tensor.matmul_mx(
                    out=bank[:, r, :],
                    lhsT=z_words[:, P * r : P * (r + 1)].bitcast(FP8X4),
                    lhsT_scale=z_scales[:, P * r : P * (r + 1)],
                    rhs=z2_words[:].bitcast(FP8X4),
                    rhs_scale=z2_scales[:],
                    start=True,
                    stop=True,
                )
            y = tile("y%d" % c, [P, PACK, CHUNK], F32)
            nc.scalar.activation(y[:], bank[:], ACT.Relu, scale=0.0625)
            nc.sync.dma_start(out_rows[:, :, c * CHUNK : (c + 1) * CHUNK], y[:])
            return y

        def hand_on(c, y):
            y_in = tile("y_in%d" % c, [P, CHUNK, PACK], BF16)
            nc.vector.tensor_copy(y_in[:], y[:].rearrange("p r n -> p n r"))
            cols = slice(c * CHUNK, (c + 1) * CHUNK)
            nc.vector.quantize_mx(
                out=y_words[:, cols].bitcast(FP8X4), scales=y_scales[:, cols], in_=y_in[:].rearrange("p n t -> p (n t)")
            )
            nc.sync.dma_start(out_words[:, cols], y_words[:, cols].bitcast(I32))

        z2_ins = [fetch(0), fetch(1)]
        nc.vector.quantize_mx(
            out=z_words[:].bitcast(FP8X4), scales=z_scales[:], in_=z_in[:].rearrange("p r m t -> p (r m t)")
        )
        ys = []
        for c in range(n_chunks):
            ys.append(score(c, z2_ins[c]))
            if c + 2 < n_chunks:
                z2_ins.append(fetch(c + 2))
        for c in range(n_chunks):
            hand_on(c, ys[c])
        for q in range(4):
            (nc.sync if q % 2 else nc.scalar).dma_start(
                out_2[0, 4 * q : 4 * q + 4, :].bitcast(I32), y_scales[32 * q : 32 * q + 4, :].bitcast(I32)
            )
